import numpy as np
import ml_dtypes


def mxq(x, axis, fmt="e4m3"):
    dtype, down = {"e4m3": (ml_dtypes.float8_e4m3fn, 7), "e5m2": (ml_dtypes.float8_e5m2, 14)}[fmt]
    v = np.moveaxis(np.asarray(x, np.float32).astype(ml_dtypes.bfloat16).astype(np.float64), axis, -1)
    blocks = v.reshape(v.shape[:-1] + (-1, 32))
    amax = np.abs(blocks).max(-1, keepdims=True)
    byte = np.maximum(np.where(amax > 0, np.frexp(amax)[1] - 1 + 127, 0) - down, 1)
    scale = np.exp2(byte - 127.0)
    codes = (blocks / scale).astype(np.float32).astype(dtype).astype(np.float64)
    return np.moveaxis((codes * scale).reshape(v.shape), -1, axis)


WIDE = False


def mx_kscale(k):
    if not WIDE:
        return np.ones(k)
    levels = np.array([10, -10, 5, -5, 0])
    if k % 512:
        return np.exp2(np.random.permutation(np.resize(levels, k // 32))).repeat(32)
    a = np.empty((k // 512, 16))
    for p in range(k // 512):
        a[p, :8] = np.random.permutation(np.resize(levels, 8))
        for g in range(8):
            far = levels[np.abs(levels - a[p, g]) >= 10]
            a[p, g + 8] = far[np.random.randint(len(far))]
    return np.exp2(a.ravel()).repeat(32)


def f64(x):
    return np.asarray(x).astype(np.float64)


def striped(idx):
    return np.tile(idx.reshape(-1, 16).T, (8, 1)).astype(np.uint16)


def unstriped(offs):
    return offs[:16].T.reshape(-1).astype(np.int64)


def pack_weight(w):
    k, n = w.shape
    w = f64(np.asarray(w, np.float32).astype(ml_dtypes.bfloat16)).reshape(k // 32, 32, n)
    amax = np.abs(w).max(1)
    byte = np.clip(np.where(amax > 0, np.frexp(amax)[1] - 1 + 127 - 7, 1), 1, 254)
    scaled = (w * np.exp2(127.0 - byte)[:, None, :]).reshape(k, n).astype(np.float32)
    words = np.ascontiguousarray(scaled.reshape(k // 512, 128, 4, n).transpose(0, 1, 3, 2)).astype(ml_dtypes.float8_e4m3fn).view(np.uint8)
    return words, np.ascontiguousarray(byte.astype(np.uint8).reshape(k // 512, 16, n))


def unpack_weight(words, scales):
    g, p, n, _ = words.shape
    vals = np.ascontiguousarray(words).view(ml_dtypes.float8_e4m3fn).astype(np.float64) * np.repeat(np.exp2(scales.astype(np.float64) - 127.0), 8, axis=1)[..., None]
    return vals.transpose(0, 1, 3, 2).reshape(g * 512, n)


K, T, E, C, N = 1024, 1024, 16, 128, 256


def by_expert(wq, xq):
    return np.concatenate([wq[e].T @ xq[:, e * C:(e + 1) * C] for e in range(E)], axis=1)


def setup_inputs():
    n = np.random.standard_normal
    s = mx_kscale(K)[:, None]
    first = np.random.permutation(np.repeat(np.arange(E), T // E))
    second = (first + 1 + np.random.permutation(np.repeat(np.arange(E - 1), -(-T // (E - 1)))[:T])) % E
    while np.bincount(second, minlength=E).max() != T // E:
        load = np.bincount(second, minlength=E); hi, lo = int(load.argmax()), int(load.argmin())
        t = np.flatnonzero((second == hi) & (first != lo))[0]; second[t] = lo
    slot_token = np.empty(E * C, np.int64); pos = np.empty((2, T), np.int64); fill = np.zeros(E, np.int64)
    place = np.stack([np.random.permutation(C) for _ in range(E)])
    for r, deal in enumerate((first, second)):
        for t in np.random.permutation(T):
            e = deal[t]; j = e * C + place[e, fill[e]]; fill[e] += 1; slot_token[j] = t; pos[r, t] = j
    g = np.random.uniform(0.2, 0.8, T)
    packed = [pack_weight(m) for m in n((E, K, N)) / np.sqrt(K) / s[None]]
    return {
        "xT": (n((K, T)) * s).astype(np.float32),
        "w_words": np.stack([m[0] for m in packed]),
        "w_scales": np.stack([m[1] for m in packed]),
        "gate": np.stack([np.tile(g, (N, 1)), np.tile(1.0 - g, (N, 1))]).astype(np.float32),
        "offs": striped(slot_token),
        "pos1": striped(pos[0]),
        "pos2": striped(pos[1]),
    }


def reference(xT, w_words, w_scales, gate, offs, pos1, pos2):
    idx = unstriped(offs)
    xq = mxq(f64(xT)[:, idx], 0, "e4m3")
    w = np.stack([unpack_weight(w_words[e], w_scales[e]) for e in range(E)])
    y = by_expert(w, xq)
    return f64(gate[0]) * y[:, unstriped(pos1)] + f64(gate[1]) * y[:, unstriped(pos2)]

@@ -1,0 +1,226 @@
+from contextlib import ExitStack
+
+import concourse.mybir as mybir
+from concourse.masks import make_identity
+
+K, T, E, C, N = 1024, 1024, 16, 128, 256
+FLOPS = 2 * K * N * E * C
+
+F32 = mybir.dt.float32
+BF16 = mybir.dt.bfloat16
+I32 = mybir.dt.int32
+U32 = mybir.dt.uint32
+U16 = mybir.dt.uint16
+U8 = mybir.dt.uint8
+FP8X4 = mybir.dt.float8_e4m3fn_x4
+MULT = mybir.AluOpType.mult
+ADD = mybir.AluOpType.add
+
+P = 128
+PACK = 4
+PASSES = K // (P * PACK)
+SLOTS = E * C
+BANK = 512
+NBANK = SLOTS // BANK
+PER_BANK = BANK // C
+X_LOADS = ((512, 512), (256, 256, 256, 256))
+SUB = 256
+SLICES = (768, 768, 512)
+LAST_CUT = 256
+PLANE = (4, 0)
+W_BOTH = ((0, 4), (4, 8))
+W_BLOCK0 = ((8, 12), (12, 16))
+W_BLOCK1 = ((8, 12), (12, 14), (14, 16))
+RUNS1 = ((0, 4, 0, 0), (4, 8, 1, 0), (8, 11, 2, 0), (11, 14, 3, 0), (14, 15, 2, 3), (15, 16, 3, 3))
+CHUNKS1 = (768, 256)
+
+
+def tile_routed_moe_kernel(tc, xT, w_words, w_scales, gate, offs, pos1, pos2, out):
+    nc = tc.nc
+    with ExitStack() as ctx:
+        lists = ctx.enter_context(tc.tile_pool(name="lists", bufs=1))
+        keep = ctx.enter_context(tc.tile_pool(name="keep", bufs=1))
+        psum = ctx.enter_context(tc.psum_pool(name="psum", bufs=1))
+
+        offs_t = lists.tile([P, SLOTS // 16], U16, name="offs_t")
+        pos_t = [lists.tile([P, T // 16], U16, name="pos%d_t" % r) for r in range(2)]
+        nc.sync.dma_start(offs_t[:], offs)
+
+        tok_bytes = keep.tile([P, T], U8, name="tok_bytes", align_bytes=64)
+        nc.gpsimd.memset(tok_bytes[:], 0)
+        ws = keep.tile([P, E * PASSES, N], U8, name="ws", align_bytes=64)
+        nc.vector.memset(ws[:].rearrange("p g n -> p (g n)").bitcast(I32), 0)
+        ident = keep.tile([P, P], F32, name="ident")
+        make_identity(nc, ident[:])
+        ones = keep.tile([P, P], F32, name="ones")
+        nc.gpsimd.memset(ones[:], 1.0)
+        gate_row = keep.tile([P, T], F32, name="gate_row")
+        nc.gpsimd.memset(gate_row[:], 0.0)
+
+        x_view = xT.rearrange("(a p j) t -> a p j t", p=P, j=PACK)
+        raw = {}
+        for a in range(PASSES):
+            t0 = 0
+            for n in X_LOADS[a]:
+                chunk = keep.tile([P, PACK, n], F32, name="raw%d_%d" % (a, t0))
+                nc.sync.dma_start(chunk[:], x_view[a][:, :, t0:t0 + n])
+                for u in range(0, n, SUB):
+                    raw[a, (t0 + u) // SUB] = chunk[:, :, u:u + SUB]
+                t0 += n
+
+        nc.sync.dma_start(gate_row[0:1, :], gate[0, 0:1, :])
+
+        s_view = w_scales.rearrange("e a (q r) n -> r q (e a) n", r=4)
+        for r in range(4):
+            nc.sync.dma_start(ws[r:P:32, :, :].bitcast(I32), s_view[r].bitcast(I32))
+
+        codes = {}
+
+        def load_codes(e0, e1, n0, n1):
+            tile_ = keep.tile([P, (e1 - e0) * PASSES, n1 - n0], I32, name="w%d_%d" % (e0, n0), align_bytes=64)
+            nc.sync.dma_start(
+                tile_[:],
+                w_words[e0:e1, :, :, n0:n1, :].rearrange("e a p n r -> p (e a) (n r)").bitcast(I32),
+            )
+            for e in range(e0, e1):
+                for b in range(n0 // P, n1 // P):
+                    for a in range(PASSES):
+                        codes[b, e, a] = tile_[:, (e - e0) * PASSES + a, b * P - n0:(b + 1) * P - n0]
+
+        for e0, e1 in W_BOTH:
+            load_codes(e0, e1, 0, N)
+        for e0, e1 in W_BLOCK0:
+            load_codes(e0, e1, 0, P)
+        nc.sync.dma_start(pos_t[0][:], pos1)
+        nc.sync.dma_start(pos_t[1][:], pos2)
+        gt = [keep.tile([P, T], F32, name="gate%d" % r) for r in range(2)]
+        nc.sync.dma_start(gt[1][:], gate[1, 0:P, :])
+        for e0, e1 in W_BLOCK1:
+            load_codes(e0, e1, P, N)
+
+        tok_words = [keep.tile([P, T], U32, name="tok_words%d" % a, align_bytes=64) for a in range(PASSES)]
+
+        def quantise_pass(a):
+            for c in range(T // SUB):
+                grouped = keep.tile([P, SUB, PACK], BF16, name="grouped%d_%d" % (a, c), align_bytes=64)
+                src = raw[a, c].rearrange("p j (c i) -> p c j i", i=4)
+                dst = grouped[:].rearrange("p (c i) j -> p c j i", i=4)
+                if a == 0 and c % 2 == 0:
+                    nc.vector.tensor_copy(out=dst, in_=src)
+                else:
+                    nc.scalar.copy(out=dst, in_=src)
+                cols = slice(c * SUB, (c + 1) * SUB)
+                nc.vector.quantize_mx(
+                    out=tok_words[a][:, cols].bitcast(FP8X4),
+                    scales=tok_bytes[PLANE[a]:P, cols],
+                    in_=grouped[:].rearrange("p t j -> p (t j)"),
+                )
+
+        starts = [sum(SLICES[:s]) for s in range(len(SLICES))]
+        slice_of = [max(s for s in range(len(SLICES)) if starts[s] <= e * C) for e in range(E)]
+        gw = {}
+        gb = {}
+
+        def gather_words(a, s, cut):
+            for lo in range(starts[s], starts[s] + SLICES[s], cut):
+                piece = keep.tile([P, cut], U32, name="gw%d_%d" % (a, lo), align_bytes=64)
+                nc.vector.tensor_copy(piece[:], tok_words[a][:].indirect(offs_t[:, lo // 16:(lo + cut) // 16]))
+                for e in range(lo // C, (lo + cut) // C):
+                    gw[a, e] = piece[:, e * C - lo:(e + 1) * C - lo]
+
+        def gather_bytes(s):
+            gb[s] = keep.tile([P, SLICES[s]], U8, name="gb%d" % s, align_bytes=64)
+            lcols = slice(starts[s] // 16, (starts[s] + SLICES[s]) // 16)
+            nc.vector.tensor_copy(gb[s][:], tok_bytes[:].indirect(offs_t[:, lcols]))
+
+        def multiply(b, e, a, dst):
+            s = slice_of[e]
+            o = e * C - starts[s]
+            nc.tensor.matmul_mx(
+                out=dst,
+                lhsT=codes[b, e, a].bitcast(FP8X4),
+                lhsT_scale=ws[:, e * PASSES + a, b * P:(b + 1) * P],
+                rhs=gw[a, e].bitcast(FP8X4),
+                rhs_scale=gb[s][PLANE[a]:P, o:o + C],
+                start=(a == 0),
+                stop=(a == PASSES - 1),
+            )
+
+        quantise_pass(0)
+        for s in range(len(SLICES)):
+            gather_words(0, s, SLICES[s])
+        quantise_pass(1)
+
+        for h in range(0, T, BANK):
+            spread = psum.tile([P, BANK], F32, name="spread%d" % h)
+            nc.tensor.matmul(out=spread[:], lhsT=ones[:], rhs=gate_row[:, h:h + BANK], start=True, stop=True)
+            nc.scalar.copy(out=gt[0][:, h:h + BANK], in_=spread[:])
+
+        y_sb = [keep.tile([P, SLOTS], F32, name="y_sb%d" % b) for b in range(2)]
+
+        acc = [psum.tile([P, PER_BANK, C], F32, name="acc%d" % i) for i in range(NBANK)]
+        y0_view = y_sb[0][:].rearrange("p (g i c) -> p i g c", i=NBANK, c=C)
+        last = len(SLICES) - 1
+        for s in range(len(SLICES)):
+            experts = [e for e in range(E) if slice_of[e] == s]
+            gather_bytes(s)
+            if s == last:
+                for e in experts:
+                    multiply(0, e, 0, acc[e % NBANK][:, e // NBANK, :])
+            gather_words(1, s, LAST_CUT if s == last else SLICES[s])
+            for e in experts:
+                for a in range(PASSES):
+                    if s != last or a > 0:
+                        multiply(0, e, a, acc[e % NBANK][:, e // NBANK, :])
+            order = sorted(range(NBANK), key=lambda i: max(e for e in experts if e % NBANK == i))
+            for n, i in enumerate(order):
+                groups = [e // NBANK for e in experts if e % NBANK == i]
+                g0, g1 = min(groups), max(groups) + 1
+                if s == last and n == NBANK - 1:
+                    nc.vector.tensor_copy(out=y0_view[:, i, g0:g1, :], in_=acc[i][:, g0:g1, :])
+                else:
+                    nc.scalar.copy(out=y0_view[:, i, g0:g1, :], in_=acc[i][:, g0:g1, :])
+
+        acc1 = [psum.tile([P, PER_BANK, C], F32, name="acc%d" % i) for i in range(NBANK)]
+        for e0, e1, i, g in RUNS1:
+            for e in range(e0, e1):
+                for a in range(PASSES):
+                    multiply(1, e, a, acc1[i][:, g + e - e0, :])
+            nc.scalar.copy(
+                out=y_sb[1][:, e0 * C:e1 * C],
+                in_=acc1[i][:, g:g + e1 - e0, :].rearrange("p g c -> p (g c)"),
+            )
+
+        def fetch(dst, b, r, t0, n):
+            nc.vector.tensor_tensor(
+                out=dst[:],
+                in0=y_sb[b][:].indirect(pos_t[r][:, t0 // 16:(t0 + n) // 16]),
+                in1=gt[r][:, t0:t0 + n],
+                op=MULT,
+            )
+
+        part0 = [keep.tile([P, T], F32, name="part0_%d" % r) for r in range(2)]
+        for r in range(2):
+            fetch(part0[r], 0, r, 0, T)
+        halves = range(T // BANK)
+        total = [psum.tile([P, BANK], F32, name="acc%d" % (NBANK - 2 + h)) for h in halves]
+        for r in range(2):
+            for h in halves:
+                nc.tensor.matmul(out=total[h][:], lhsT=ident[:], rhs=part0[r][:, h * BANK:(h + 1) * BANK], start=(r == 0), stop=(r == 1))
+        for h in halves:
+            res0 = keep.tile([P, BANK], F32, name="res0_%d" % h)
+            nc.scalar.copy(out=res0[:], in_=total[h][:])
+            nc.sync.dma_start(out[0:P, h * BANK:(h + 1) * BANK], res0[:])
+
+        n0, n1 = CHUNKS1
+        res1 = [keep.tile([P, n], F32, name="res1_%d" % i) for i, n in enumerate(CHUNKS1)]
+        pa = [keep.tile([P, n0], F32, name="pa%d" % r) for r in range(2)]
+        pb = [keep.tile([P, n1], F32, name="pb%d" % r) for r in range(2)]
+        fetch(pa[0], 1, 0, 0, n0)
+        fetch(pa[1], 1, 1, 0, n0)
+        fetch(pb[0], 1, 0, n0, n1)
+        nc.vector.tensor_tensor(out=res1[0][:], in0=pa[0][:], in1=pa[1][:], op=ADD)
+        nc.sync.dma_start(out[P:2 * P, 0:n0], res1[0][:])
+        fetch(pb[1], 1, 1, n0, n1)
+        nc.vector.tensor_tensor(out=res1[1][:], in0=pb[0][:], in1=pb[1][:], op=ADD)
+        nc.sync.dma_start(out[P:2 * P, n0:T], res1[1][:])

@@ -27,7 +27,8 @@ X_LOADS = ((512, 512), (256, 256, 256, 256))
 SUB = 256
 SLICES = (768, 768, 512)
 LAST_CUT = 256
-PLANE = (4, 0)
+PLANE = (0, 12)
+W_PLANES = 4
 W_BOTH = ((0, 4), (4, 8))
 W_BLOCK0 = ((8, 12), (12, 16))
 W_BLOCK1 = ((8, 12), (12, 14), (14, 16))
@@ -48,7 +49,7 @@ def tile_routed_moe_kernel(tc, xT, w_words, w_scales, gate, offs, pos1, pos2, ou
 
         tok_bytes = keep.tile([P, T], U8, name="tok_bytes", align_bytes=64)
         nc.gpsimd.memset(tok_bytes[:], 0)
-        ws = keep.tile([P, E * PASSES, N], U8, name="ws", align_bytes=64)
+        ws = keep.tile([P, E * PASSES // W_PLANES, N], U8, name="ws", align_bytes=64)
         nc.vector.memset(ws[:].rearrange("p g n -> p (g n)").bitcast(I32), 0)
         ident = keep.tile([P, P], F32, name="ident")
         make_identity(nc, ident[:])
@@ -70,9 +71,10 @@ def tile_routed_moe_kernel(tc, xT, w_words, w_scales, gate, offs, pos1, pos2, ou
 
         nc.sync.dma_start(gate_row[0:1, :], gate[0, 0:1, :])
 
-        s_view = w_scales.rearrange("e a (q r) n -> r q (e a) n", r=4)
-        for r in range(4):
-            nc.sync.dma_start(ws[r:P:32, :, :].bitcast(I32), s_view[r].bitcast(I32))
+        s_view = w_scales.rearrange("(g f) a (q r) n -> (f a) r q g n", f=2, r=4)
+        for r in (0, 2, 1, 3):
+            for f in range(W_PLANES):
+                nc.sync.dma_start(ws[4 * f + r:P:32, :, :].bitcast(I32), s_view[f, r].bitcast(I32))
 
         codes = {}
 
@@ -139,7 +141,7 @@ def tile_routed_moe_kernel(tc, xT, w_words, w_scales, gate, offs, pos1, pos2, ou
             nc.tensor.matmul_mx(
                 out=dst,
                 lhsT=codes[b, e, a].bitcast(FP8X4),
-                lhsT_scale=ws[:, e * PASSES + a, b * P:(b + 1) * P],
+                lhsT_scale=ws[4 * (PASSES * (e % 2) + a):P, e // 2, b * P:(b + 1) * P],
                 rhs=gw[a, e].bitcast(FP8X4),
                 rhs_scale=gb[s][PLANE[a]:P, o:o + C],
                 start=(a == 0),

@@ -32,7 +32,8 @@ W_PLANES = 4
 W_BOTH = ((0, 4), (4, 8))
 W_BLOCK0 = ((8, 12), (12, 16))
 W_BLOCK1 = ((8, 12), (12, 14), (14, 16))
-RUNS1 = ((0, 4, 0, 0), (4, 8, 1, 0), (8, 11, 2, 0), (11, 14, 3, 0), (14, 15, 2, 3), (15, 16, 3, 3))
+EARLY = 8
+RUNS1 = ((8, 11, 2, 0), (11, 14, 3, 0), (14, 15, 2, 3), (15, 16, 3, 3))
 CHUNKS1 = (768, 256)
 
 
@@ -163,6 +164,7 @@ def tile_routed_moe_kernel(tc, xT, w_words, w_scales, gate, offs, pos1, pos2, ou
         acc = [psum.tile([P, PER_BANK, C], F32, name="acc%d" % i) for i in range(NBANK)]
         y0_view = y_sb[0][:].rearrange("p (g i c) -> p i g c", i=NBANK, c=C)
         last = len(SLICES) - 1
+        early = [psum.tile([P, PER_BANK, C], F32, name="early%d" % i) for i in range(EARLY // PER_BANK)]
         for s in range(len(SLICES)):
             experts = [e for e in range(E) if slice_of[e] == s]
             gather_bytes(s)
@@ -182,8 +184,19 @@ def tile_routed_moe_kernel(tc, xT, w_words, w_scales, gate, offs, pos1, pos2, ou
                     nc.vector.tensor_copy(out=y0_view[:, i, g0:g1, :], in_=acc[i][:, g0:g1, :])
                 else:
                     nc.scalar.copy(out=y0_view[:, i, g0:g1, :], in_=acc[i][:, g0:g1, :])
+            soon = [e for e in experts if e < EARLY]
+            for e in soon:
+                for a in range(PASSES):
+                    multiply(1, e, a, early[e // PER_BANK][:, e % PER_BANK, :])
+            for i in range(len(early)):
+                mine = [e for e in soon if e // PER_BANK == i]
+                if mine:
+                    nc.scalar.copy(
+                        out=y_sb[1][:, mine[0] * C:(mine[-1] + 1) * C],
+                        in_=early[i][:, mine[0] % PER_BANK:mine[-1] % PER_BANK + 1, :].rearrange("p g c -> p (g c)"),
+                    )
 
-        acc1 = [psum.tile([P, PER_BANK, C], F32, name="acc%d" % i) for i in range(NBANK)]
+        acc1 = [None, None] + [psum.tile([P, PER_BANK, C], F32, name="acc%d" % i) for i in (2, 3)]
         for e0, e1, i, g in RUNS1:
             for e in range(e0, e1):
                 for a in range(PASSES):

@@ -25,6 +25,7 @@ NBANK = SLOTS // BANK
 PER_BANK = BANK // C
 X_LOADS = ((512, 512), (256, 256, 256, 256))
 SUB = 256
+QUANT = (256, 512)
 SLICES = (768, 768, 512)
 LAST_CUT = 256
 PLANE = (0, 12)
@@ -46,7 +47,6 @@ def tile_routed_moe_kernel(tc, xT, w_words, w_scales, gate, offs, pos1, pos2, ou
 
         offs_t = lists.tile([P, SLOTS // 16], U16, name="offs_t")
         pos_t = [lists.tile([P, T // 16], U16, name="pos%d_t" % r) for r in range(2)]
-        nc.sync.dma_start(offs_t[:], offs)
 
         tok_bytes = keep.tile([P, T], U8, name="tok_bytes", align_bytes=64)
         nc.gpsimd.memset(tok_bytes[:], 0)
@@ -69,6 +69,8 @@ def tile_routed_moe_kernel(tc, xT, w_words, w_scales, gate, offs, pos1, pos2, ou
                 for u in range(0, n, SUB):
                     raw[a, (t0 + u) // SUB] = chunk[:, :, u:u + SUB]
                 t0 += n
+            if a == 0:
+                nc.sync.dma_start(offs_t[:], offs)
 
         nc.sync.dma_start(gate_row[0:1, :], gate[0, 0:1, :])
 
@@ -104,15 +106,17 @@ def tile_routed_moe_kernel(tc, xT, w_words, w_scales, gate, offs, pos1, pos2, ou
         tok_words = [keep.tile([P, T], U32, name="tok_words%d" % a, align_bytes=64) for a in range(PASSES)]
 
         def quantise_pass(a):
-            for c in range(T // SUB):
-                grouped = keep.tile([P, SUB, PACK], BF16, name="grouped%d_%d" % (a, c), align_bytes=64)
-                src = raw[a, c].rearrange("p j (c i) -> p c j i", i=4)
-                dst = grouped[:].rearrange("p (c i) j -> p c j i", i=4)
-                if a == 0 and c % 2 == 0:
-                    nc.vector.tensor_copy(out=dst, in_=src)
-                else:
-                    nc.scalar.copy(out=dst, in_=src)
-                cols = slice(c * SUB, (c + 1) * SUB)
+            wide = QUANT[a]
+            for c0 in range(0, T // SUB, wide // SUB):
+                grouped = keep.tile([P, wide, PACK], BF16, name="grouped%d_%d" % (a, c0), align_bytes=64)
+                for c in range(c0, c0 + wide // SUB):
+                    src = raw[a, c].rearrange("p j (c i) -> p c j i", i=4)
+                    dst = grouped[:, (c - c0) * SUB:(c - c0 + 1) * SUB, :].rearrange("p (c i) j -> p c j i", i=4)
+                    if a == 0 and c % 2 == 0:
+                        nc.vector.tensor_copy(out=dst, in_=src)
+                    else:
+                        nc.scalar.copy(out=dst, in_=src)
+                cols = slice(c0 * SUB, c0 * SUB + wide)
                 nc.vector.quantize_mx(
                     out=tok_words[a][:, cols].bitcast(FP8X4),
                     scales=tok_bytes[PLANE[a]:P, cols],

@@ -23,8 +23,9 @@ SLOTS = E * C
 BANK = 512
 NBANK = SLOTS // BANK
 PER_BANK = BANK // C
-X_LOADS = ((512, 512), (256, 256, 256, 256))
+X_LOADS = ((512, 256, 256), (256, 256, 256, 256))
 SUB = 256
+BY_VECTOR = ((256, 0, 128, 160), (0, 0, 0, 0))
 QUANT = (256, 512)
 SLICES = (768, 768, 512)
 LAST_CUT = 256
@@ -112,10 +113,11 @@ def tile_routed_moe_kernel(tc, xT, w_words, w_scales, gate, offs, pos1, pos2, ou
                 for c in range(c0, c0 + wide // SUB):
                     src = raw[a, c].rearrange("p j (c i) -> p c j i", i=4)
                     dst = grouped[:, (c - c0) * SUB:(c - c0 + 1) * SUB, :].rearrange("p (c i) j -> p c j i", i=4)
-                    if a == 0 and c % 2 == 0:
-                        nc.vector.tensor_copy(out=dst, in_=src)
-                    else:
-                        nc.scalar.copy(out=dst, in_=src)
+                    mine = BY_VECTOR[a][c] // 4
+                    if mine > 0:
+                        nc.vector.tensor_copy(out=dst[:, 0:mine], in_=src[:, 0:mine])
+                    if mine < SUB // 4:
+                        nc.scalar.copy(out=dst[:, mine:], in_=src[:, mine:])
                 cols = slice(c0 * SUB, c0 * SUB + wide)
                 nc.vector.quantize_mx(
                     out=tok_words[a][:, cols].bitcast(FP8X4),

@@ -23,10 +23,11 @@ SLOTS = E * C
 BANK = 512
 NBANK = SLOTS // BANK
 PER_BANK = BANK // C
-X_LOADS = ((512, 256, 256), (256, 256, 256, 256))
-SUB = 256
-BY_VECTOR = ((256, 0, 128, 160), (0, 0, 0, 0))
-QUANT = (256, 512)
+X_LOADS = ((640, 384), (256, 256, 256, 256))
+QUANT = (
+    (((256, 256),), ((256, 0),), ((128, 64),), ((256, 128),), ((128, 80),)),
+    (((256, 0), (256, 0)), ((256, 0), (256, 0))),
+)
 SLICES = (768, 768, 512)
 LAST_CUT = 256
 PLANE = (0, 12)
@@ -67,8 +68,7 @@ def tile_routed_moe_kernel(tc, xT, w_words, w_scales, gate, offs, pos1, pos2, ou
             for n in X_LOADS[a]:
                 chunk = keep.tile([P, PACK, n], F32, name="raw%d_%d" % (a, t0))
                 nc.sync.dma_start(chunk[:], x_view[a][:, :, t0:t0 + n])
-                for u in range(0, n, SUB):
-                    raw[a, (t0 + u) // SUB] = chunk[:, :, u:u + SUB]
+                raw[a, t0] = chunk
                 t0 += n
             if a == 0:
                 nc.sync.dma_start(offs_t[:], offs)
@@ -106,24 +106,32 @@ def tile_routed_moe_kernel(tc, xT, w_words, w_scales, gate, offs, pos1, pos2, ou
 
         tok_words = [keep.tile([P, T], U32, name="tok_words%d" % a, align_bytes=64) for a in range(PASSES)]
 
+        def raw_tokens(a, t0, n):
+            first = max(t for b, t in raw if b == a and t <= t0)
+            return raw[a, first][:, :, t0 - first:t0 - first + n]
+
         def quantise_pass(a):
-            wide = QUANT[a]
-            for c0 in range(0, T // SUB, wide // SUB):
-                grouped = keep.tile([P, wide, PACK], BF16, name="grouped%d_%d" % (a, c0), align_bytes=64)
-                for c in range(c0, c0 + wide // SUB):
-                    src = raw[a, c].rearrange("p j (c i) -> p c j i", i=4)
-                    dst = grouped[:, (c - c0) * SUB:(c - c0 + 1) * SUB, :].rearrange("p (c i) j -> p c j i", i=4)
-                    mine = BY_VECTOR[a][c] // 4
-                    if mine > 0:
-                        nc.vector.tensor_copy(out=dst[:, 0:mine], in_=src[:, 0:mine])
-                    if mine < SUB // 4:
-                        nc.scalar.copy(out=dst[:, mine:], in_=src[:, mine:])
-                cols = slice(c0 * SUB, c0 * SUB + wide)
+            t0 = 0
+            for copies in QUANT[a]:
+                wide = sum(n for n, by_vector in copies)
+                grouped = keep.tile([P, wide, PACK], BF16, name="grouped%d_%d" % (a, t0), align_bytes=64)
+                done = 0
+                for n, by_vector in copies:
+                    src = raw_tokens(a, t0 + done, n).rearrange("p j (c i) -> p c j i", i=4)
+                    dst = grouped[:, done:done + n, :].rearrange("p (c i) j -> p c j i", i=4)
+                    cut = by_vector // 4
+                    if by_vector > 0:
+                        nc.vector.tensor_copy(out=dst[:, :cut], in_=src[:, :cut])
+                    if by_vector < n:
+                        nc.scalar.copy(out=dst[:, cut:], in_=src[:, cut:])
+                    done += n
+                cols = slice(t0, t0 + wide)
                 nc.vector.quantize_mx(
                     out=tok_words[a][:, cols].bitcast(FP8X4),
                     scales=tok_bytes[PLANE[a]:P, cols],
                     in_=grouped[:].rearrange("p t j -> p (t j)"),
                 )
+                t0 += wide
 
         starts = [sum(SLICES[:s]) for s in range(len(SLICES))]
         slice_of = [max(s for s in range(len(SLICES)) if starts[s] <= e * C) for e in range(E)]

@@ -37,7 +37,8 @@ W_BLOCK0 = ((8, 12), (12, 16))
 W_BLOCK1 = ((8, 12), (12, 14), (14, 16))
 EARLY = 8
 RUNS1 = ((8, 11, 2, 0), (11, 14, 3, 0), (14, 15, 2, 3), (15, 16, 3, 3))
-CHUNKS1 = (768, 256)
+SUM1 = 384
+CHUNKS1 = (384, 256)
 
 
 def tile_routed_moe_kernel(tc, xT, w_words, w_scales, gate, offs, pos1, pos2, out):
@@ -56,10 +57,6 @@ def tile_routed_moe_kernel(tc, xT, w_words, w_scales, gate, offs, pos1, pos2, ou
         nc.vector.memset(ws[:].rearrange("p g n -> p (g n)").bitcast(I32), 0)
         ident = keep.tile([P, P], F32, name="ident")
         make_identity(nc, ident[:])
-        ones = keep.tile([P, P], F32, name="ones")
-        nc.gpsimd.memset(ones[:], 1.0)
-        gate_row = keep.tile([P, T], F32, name="gate_row")
-        nc.gpsimd.memset(gate_row[:], 0.0)
 
         x_view = xT.rearrange("(a p j) t -> a p j t", p=P, j=PACK)
         raw = {}
@@ -72,8 +69,6 @@ def tile_routed_moe_kernel(tc, xT, w_words, w_scales, gate, offs, pos1, pos2, ou
                 t0 += n
             if a == 0:
                 nc.sync.dma_start(offs_t[:], offs)
-
-        nc.sync.dma_start(gate_row[0:1, :], gate[0, 0:1, :])
 
         s_view = w_scales.rearrange("(g f) a (q r) n -> (f a) r q g n", f=2, r=4)
         for r in (0, 2, 1, 3):
@@ -100,7 +95,8 @@ def tile_routed_moe_kernel(tc, xT, w_words, w_scales, gate, offs, pos1, pos2, ou
         nc.sync.dma_start(pos_t[0][:], pos1)
         nc.sync.dma_start(pos_t[1][:], pos2)
         gt = [keep.tile([P, T], F32, name="gate%d" % r) for r in range(2)]
-        nc.sync.dma_start(gt[1][:], gate[1, 0:P, :])
+        for r in range(2):
+            nc.sync.dma_start(gt[r][:], gate[r, 0:P, :])
         for e0, e1 in W_BLOCK1:
             load_codes(e0, e1, P, N)
 
@@ -168,11 +164,6 @@ def tile_routed_moe_kernel(tc, xT, w_words, w_scales, gate, offs, pos1, pos2, ou
             gather_words(0, s, SLICES[s])
         quantise_pass(1)
 
-        for h in range(0, T, BANK):
-            spread = psum.tile([P, BANK], F32, name="spread%d" % h)
-            nc.tensor.matmul(out=spread[:], lhsT=ones[:], rhs=gate_row[:, h:h + BANK], start=True, stop=True)
-            nc.scalar.copy(out=gt[0][:, h:h + BANK], in_=spread[:])
-
         y_sb = [keep.tile([P, SLOTS], F32, name="y_sb%d" % b) for b in range(2)]
 
         acc = [psum.tile([P, PER_BANK, C], F32, name="acc%d" % i) for i in range(NBANK)]
@@ -220,36 +211,42 @@ def tile_routed_moe_kernel(tc, xT, w_words, w_scales, gate, offs, pos1, pos2, ou
                 in_=acc1[i][:, g:g + e1 - e0, :].rearrange("p g c -> p (g c)"),
             )
 
-        def fetch(dst, b, r, t0, n):
+        def fetch(b, r, t0, n):
+            part = keep.tile([P, n], F32, name="part%d_%d_%d" % (b, r, t0))
             nc.vector.tensor_tensor(
-                out=dst[:],
+                out=part[:],
                 in0=y_sb[b][:].indirect(pos_t[r][:, t0 // 16:(t0 + n) // 16]),
                 in1=gt[r][:, t0:t0 + n],
                 op=MULT,
             )
+            return part
 
-        part0 = [keep.tile([P, T], F32, name="part0_%d" % r) for r in range(2)]
-        for r in range(2):
-            fetch(part0[r], 0, r, 0, T)
-        halves = range(T // BANK)
-        total = [psum.tile([P, BANK], F32, name="acc%d" % (NBANK - 2 + h)) for h in halves]
-        for r in range(2):
-            for h in halves:
-                nc.tensor.matmul(out=total[h][:], lhsT=ident[:], rhs=part0[r][:, h * BANK:(h + 1) * BANK], start=(r == 0), stop=(r == 1))
-        for h in halves:
-            res0 = keep.tile([P, BANK], F32, name="res0_%d" % h)
-            nc.scalar.copy(out=res0[:], in_=total[h][:])
-            nc.sync.dma_start(out[0:P, h * BANK:(h + 1) * BANK], res0[:])
+        def add_product(total, part, r):
+            nc.tensor.matmul(out=total[:], lhsT=ident[:], rhs=part, start=(r == 0), stop=(r == 1))
 
-        n0, n1 = CHUNKS1
-        res1 = [keep.tile([P, n], F32, name="res1_%d" % i) for i, n in enumerate(CHUNKS1)]
-        pa = [keep.tile([P, n0], F32, name="pa%d" % r) for r in range(2)]
-        pb = [keep.tile([P, n1], F32, name="pb%d" % r) for r in range(2)]
-        fetch(pa[0], 1, 0, 0, n0)
-        fetch(pa[1], 1, 1, 0, n0)
-        fetch(pb[0], 1, 0, n0, n1)
-        nc.vector.tensor_tensor(out=res1[0][:], in0=pa[0][:], in1=pa[1][:], op=ADD)
-        nc.sync.dma_start(out[P:2 * P, 0:n0], res1[0][:])
-        fetch(pb[1], 1, 1, n0, n1)
-        nc.vector.tensor_tensor(out=res1[1][:], in0=pb[0][:], in1=pb[1][:], op=ADD)
-        nc.sync.dma_start(out[P:2 * P, n0:T], res1[1][:])
+        def store_total(total, b, t0, n):
+            res = keep.tile([P, n], F32, name="res%d_%d" % (b, t0))
+            nc.scalar.copy(out=res[:], in_=total[:])
+            nc.scalar.dma_start(out[b * P:(b + 1) * P, t0:t0 + n], res[:])
+
+        halves = range(0, T, BANK)
+        total0 = {t0: psum.tile([P, BANK], F32, name="acc%d" % (NBANK - 2 + t0 // BANK)) for t0 in halves}
+        for r in range(2):
+            part = fetch(0, r, 0, T)
+            for t0 in halves:
+                add_product(total0[t0], part[:, t0:t0 + BANK], r)
+        for t0 in halves:
+            store_total(total0[t0], 0, t0, BANK)
+
+        total1 = psum.tile([P, SUM1], F32, name="total1")
+        first = fetch(1, 0, 0, T)
+        add_product(total1, first[:, 0:SUM1], 0)
+        add_product(total1, fetch(1, 1, 0, SUM1)[:], 1)
+        store_total(total1, 1, 0, SUM1)
+        t0 = SUM1
+        for n in CHUNKS1:
+            second = fetch(1, 1, t0, n)
+            res = keep.tile([P, n], F32, name="res1_%d" % t0)
+            nc.vector.tensor_tensor(out=res[:], in0=first[:, t0:t0 + n], in1=second[:], op=ADD)
+            nc.sync.dma_start(out[P:2 * P, t0:t0 + n], res[:])
+            t0 += n

@@ -30,6 +30,7 @@ QUANT = (
 )
 SLICES = (768, 768, 512)
 LAST_CUT = 256
+GATE_ROWS = T // P
 PLANE = (0, 12)
 W_PLANES = 4
 W_BOTH = ((0, 4), (4, 8))
@@ -57,6 +58,8 @@ def tile_routed_moe_kernel(tc, xT, w_words, w_scales, gate, offs, pos1, pos2, ou
         nc.vector.memset(ws[:].rearrange("p g n -> p (g n)").bitcast(I32), 0)
         ident = keep.tile([P, P], F32, name="ident")
         make_identity(nc, ident[:])
+        gate_rows = keep.tile([P, P], F32, name="gate_rows")
+        nc.gpsimd.memset(gate_rows[:], 0.0)
 
         x_view = xT.rearrange("(a p j) t -> a p j t", p=P, j=PACK)
         raw = {}
@@ -69,6 +72,9 @@ def tile_routed_moe_kernel(tc, xT, w_words, w_scales, gate, offs, pos1, pos2, ou
                 t0 += n
             if a == 0:
                 nc.sync.dma_start(offs_t[:], offs)
+
+        for r in range(2):
+            nc.sync.dma_start(gate_rows[GATE_ROWS * r:GATE_ROWS * (r + 1), :], gate[r, 0, :].rearrange("(h c) -> h c", c=P))
 
         s_view = w_scales.rearrange("(g f) a (q r) n -> (f a) r q g n", f=2, r=4)
         for r in (0, 2, 1, 3):
@@ -94,9 +100,6 @@ def tile_routed_moe_kernel(tc, xT, w_words, w_scales, gate, offs, pos1, pos2, ou
             load_codes(e0, e1, 0, P)
         nc.sync.dma_start(pos_t[0][:], pos1)
         nc.sync.dma_start(pos_t[1][:], pos2)
-        gt = [keep.tile([P, T], F32, name="gate%d" % r) for r in range(2)]
-        for r in range(2):
-            nc.sync.dma_start(gt[r][:], gate[r, 0:P, :])
         for e0, e1 in W_BLOCK1:
             load_codes(e0, e1, P, N)
 
@@ -163,6 +166,18 @@ def tile_routed_moe_kernel(tc, xT, w_words, w_scales, gate, offs, pos1, pos2, ou
         for s in range(len(SLICES)):
             gather_words(0, s, SLICES[s])
         quantise_pass(1)
+
+        gate_cols = keep.tile([P, 2 * GATE_ROWS], F32, name="gate_cols")
+        turned = psum.tile([P, P], F32, name="spare0")
+        nc.tensor.transpose(turned[:], gate_rows[:], ident[:])
+        nc.scalar.copy(out=gate_cols[:], in_=turned[:, 0:2 * GATE_ROWS])
+        gt = [keep.tile([P, T], F32, name="gate%d" % r) for r in range(2)]
+        for q in range(2 * T // BANK):
+            spread = psum.tile([P, BANK], F32, name="spare%d" % ((q + 1) % 2))
+            for i in range(BANK // P):
+                m = q * (BANK // P) + i
+                nc.tensor.transpose(spread[:, i * P:(i + 1) * P], gate_cols[:, m:m + 1].to_broadcast([P, P]), ident[:])
+            nc.scalar.copy(out=gt[q * BANK // T][:, q * BANK % T:q * BANK % T + BANK], in_=spread[:])
 
         y_sb = [keep.tile([P, SLOTS], F32, name="y_sb%d" % b) for b in range(2)]
 
@@ -238,7 +253,7 @@ def tile_routed_moe_kernel(tc, xT, w_words, w_scales, gate, offs, pos1, pos2, ou
         for t0 in halves:
             store_total(total0[t0], 0, t0, BANK)
 
-        total1 = psum.tile([P, SUM1], F32, name="total1")
+        total1 = psum.tile([P, SUM1], F32, name="spare0")
         first = fetch(1, 0, 0, T)
         add_product(total1, first[:, 0:SUM1], 0)
         add_product(total1, fetch(1, 1, 0, SUM1)[:], 1)

@@ -38,8 +38,8 @@ W_BLOCK0 = ((8, 12), (12, 16))
 W_BLOCK1 = ((8, 12), (12, 14), (14, 16))
 EARLY = 8
 RUNS1 = ((8, 11, 2, 0), (11, 14, 3, 0), (14, 15, 2, 3), (15, 16, 3, 3))
-SUM1 = 384
-CHUNKS1 = (384, 256)
+SUM1 = 448
+CHUNKS1 = (320, 256)
 
 
 def tile_routed_moe_kernel(tc, xT, w_words, w_scales, gate, offs, pos1, pos2, out):
@@ -197,13 +197,10 @@ def tile_routed_moe_kernel(tc, xT, w_words, w_scales, gate, offs, pos1, pos2, ou
                     if s != last or a > 0:
                         multiply(0, e, a, acc[e % NBANK][:, e // NBANK, :])
             order = sorted(range(NBANK), key=lambda i: max(e for e in experts if e % NBANK == i))
-            for n, i in enumerate(order):
+            for i in order:
                 groups = [e // NBANK for e in experts if e % NBANK == i]
                 g0, g1 = min(groups), max(groups) + 1
-                if s == last and n == NBANK - 1:
-                    nc.vector.tensor_copy(out=y0_view[:, i, g0:g1, :], in_=acc[i][:, g0:g1, :])
-                else:
-                    nc.scalar.copy(out=y0_view[:, i, g0:g1, :], in_=acc[i][:, g0:g1, :])
+                nc.scalar.copy(out=y0_view[:, i, g0:g1, :], in_=acc[i][:, g0:g1, :])
             soon = [e for e in experts if e < EARLY]
             for e in soon:
                 for a in range(PASSES):
@@ -247,9 +244,8 @@ def tile_routed_moe_kernel(tc, xT, w_words, w_scales, gate, offs, pos1, pos2, ou
         halves = range(0, T, BANK)
         total0 = {t0: psum.tile([P, BANK], F32, name="acc%d" % (NBANK - 2 + t0 // BANK)) for t0 in halves}
         for r in range(2):
-            part = fetch(0, r, 0, T)
             for t0 in halves:
-                add_product(total0[t0], part[:, t0:t0 + BANK], r)
+                add_product(total0[t0], fetch(0, r, t0, BANK)[:], r)
         for t0 in halves:
             store_total(total0[t0], 0, t0, BANK)
 
@@ -258,10 +254,9 @@ def tile_routed_moe_kernel(tc, xT, w_words, w_scales, gate, offs, pos1, pos2, ou
         add_product(total1, first[:, 0:SUM1], 0)
         add_product(total1, fetch(1, 1, 0, SUM1)[:], 1)
         store_total(total1, 1, 0, SUM1)
-        t0 = SUM1
-        for n in CHUNKS1:
-            second = fetch(1, 1, t0, n)
+        cuts = [(SUM1 + sum(CHUNKS1[:i]), n) for i, n in enumerate(CHUNKS1)]
+        second = [fetch(1, 1, t0, n) for t0, n in cuts]
+        for (t0, n), part in zip(cuts, second):
             res = keep.tile([P, n], F32, name="res1_%d" % t0)
-            nc.vector.tensor_tensor(out=res[:], in0=first[:, t0:t0 + n], in1=second[:], op=ADD)
+            nc.vector.tensor_tensor(out=res[:], in0=first[:, t0:t0 + n], in1=part[:], op=ADD)
             nc.sync.dma_start(out[P:2 * P, t0:t0 + n], res[:])
-            t0 += n

@@ -23,13 +23,13 @@ SLOTS = E * C
 BANK = 512
 NBANK = SLOTS // BANK
 PER_BANK = BANK // C
-X_LOADS = ((640, 384), (256, 256, 256, 256))
+X_LOADS = ((640, 384), (384, 384, 256))
 QUANT = (
     (((256, 256),), ((256, 0),), ((128, 64),), ((256, 128),), ((128, 80),)),
-    (((256, 0), (256, 0)), ((256, 0), (256, 0))),
+    (((384, 0), (128, 0)), ((256, 0), (256, 0))),
 )
 SLICES = (768, 768, 512)
-LAST_CUT = 256
+LAST_CUTS = (384, 128)
 GATE_ROWS = T // P
 PLANE = (0, 12)
 W_PLANES = 4
@@ -137,8 +137,9 @@ def tile_routed_moe_kernel(tc, xT, w_words, w_scales, gate, offs, pos1, pos2, ou
         gw = {}
         gb = {}
 
-        def gather_words(a, s, cut):
-            for lo in range(starts[s], starts[s] + SLICES[s], cut):
+        def gather_words(a, s, cuts):
+            for i, cut in enumerate(cuts):
+                lo = starts[s] + sum(cuts[:i])
                 piece = keep.tile([P, cut], U32, name="gw%d_%d" % (a, lo), align_bytes=64)
                 nc.vector.tensor_copy(piece[:], tok_words[a][:].indirect(offs_t[:, lo // 16:(lo + cut) // 16]))
                 for e in range(lo // C, (lo + cut) // C):
@@ -164,7 +165,7 @@ def tile_routed_moe_kernel(tc, xT, w_words, w_scales, gate, offs, pos1, pos2, ou
 
         quantise_pass(0)
         for s in range(len(SLICES)):
-            gather_words(0, s, SLICES[s])
+            gather_words(0, s, (SLICES[s],))
         quantise_pass(1)
 
         gate_cols = keep.tile([P, 2 * GATE_ROWS], F32, name="gate_cols")
@@ -191,16 +192,19 @@ def tile_routed_moe_kernel(tc, xT, w_words, w_scales, gate, offs, pos1, pos2, ou
             if s == last:
                 for e in experts:
                     multiply(0, e, 0, acc[e % NBANK][:, e // NBANK, :])
-            gather_words(1, s, LAST_CUT if s == last else SLICES[s])
+            gather_words(1, s, LAST_CUTS if s == last else (SLICES[s],))
             for e in experts:
                 for a in range(PASSES):
                     if s != last or a > 0:
                         multiply(0, e, a, acc[e % NBANK][:, e // NBANK, :])
             order = sorted(range(NBANK), key=lambda i: max(e for e in experts if e % NBANK == i))
-            for i in order:
+            for n, i in enumerate(order):
                 groups = [e // NBANK for e in experts if e % NBANK == i]
                 g0, g1 = min(groups), max(groups) + 1
-                nc.scalar.copy(out=y0_view[:, i, g0:g1, :], in_=acc[i][:, g0:g1, :])
+                if s == last and n == NBANK - 1:
+                    nc.vector.tensor_copy(out=y0_view[:, i, g0:g1, :], in_=acc[i][:, g0:g1, :])
+                else:
+                    nc.scalar.copy(out=y0_view[:, i, g0:g1, :], in_=acc[i][:, g0:g1, :])
             soon = [e for e in experts if e < EARLY]
             for e in soon:
                 for a in range(PASSES):
@@ -250,13 +254,13 @@ def tile_routed_moe_kernel(tc, xT, w_words, w_scales, gate, offs, pos1, pos2, ou
             store_total(total0[t0], 0, t0, BANK)
 
         total1 = psum.tile([P, SUM1], F32, name="spare0")
-        first = fetch(1, 0, 0, T)
-        add_product(total1, first[:, 0:SUM1], 0)
-        add_product(total1, fetch(1, 1, 0, SUM1)[:], 1)
+        for r in range(2):
+            add_product(total1, fetch(1, r, 0, SUM1)[:], r)
         store_total(total1, 1, 0, SUM1)
+        first = fetch(1, 0, SUM1, T - SUM1)
         cuts = [(SUM1 + sum(CHUNKS1[:i]), n) for i, n in enumerate(CHUNKS1)]
         second = [fetch(1, 1, t0, n) for t0, n in cuts]
         for (t0, n), part in zip(cuts, second):
             res = keep.tile([P, n], F32, name="res1_%d" % t0)
-            nc.vector.tensor_tensor(out=res[:], in0=first[:, t0:t0 + n], in1=part[:], op=ADD)
+            nc.vector.tensor_tensor(out=res[:], in0=first[:, t0 - SUM1:t0 - SUM1 + n], in1=part[:], op=ADD)
             nc.sync.dma_start(out[P:2 * P, t0:t0 + n], res[:])

@@ -25,8 +25,8 @@ NBANK = SLOTS // BANK
 PER_BANK = BANK // C
 X_LOADS = ((640, 384), (384, 384, 256))
 QUANT = (
-    (((256, 256),), ((256, 0),), ((128, 64),), ((256, 128),), ((128, 80),)),
-    (((384, 0), (128, 0)), ((256, 0), (256, 0))),
+    (((256, 256),), ((256, 0),), ((128, 128),), ((256, 160),), ((128, 80),)),
+    (((384, 0), (128, 0)), ((256, 0),), ((256, 0),)),
 )
 SLICES = (768, 768, 512)
 LAST_CUTS = (384, 128)

from contextlib import ExitStack

import concourse.mybir as mybir
from concourse.masks import make_identity

K, T, E, C, N = 1024, 1024, 16, 128, 256
FLOPS = 2 * K * N * E * C

F32 = mybir.dt.float32
BF16 = mybir.dt.bfloat16
I32 = mybir.dt.int32
U32 = mybir.dt.uint32
U16 = mybir.dt.uint16
U8 = mybir.dt.uint8
FP8X4 = mybir.dt.float8_e4m3fn_x4
MULT = mybir.AluOpType.mult
ADD = mybir.AluOpType.add

P = 128
PACK = 4
PASSES = K // (P * PACK)
SLOTS = E * C
BANK = 512
NBANK = SLOTS // BANK
PER_BANK = BANK // C
X_LOADS = ((640, 384), (384, 384, 256))
QUANT = (
    (((256, 256),), ((256, 0),), ((128, 128),), ((256, 160),), ((128, 80),)),
    (((384, 0), (128, 0)), ((256, 0),), ((256, 0),)),
)
SLICES = (768, 768, 512)
LAST_CUTS = (384, 128)
GATE_ROWS = T // P
PLANE = (0, 12)
W_PLANES = 4
W_BOTH = ((0, 4), (4, 8))
W_BLOCK0 = ((8, 12), (12, 16))
W_BLOCK1 = ((8, 12), (12, 14), (14, 16))
EARLY = 8
RUNS1 = ((8, 11, 2, 0), (11, 14, 3, 0), (14, 15, 2, 3), (15, 16, 3, 3))
SUM1 = 448
CHUNKS1 = (320, 256)


def tile_routed_moe_kernel(tc, xT, w_words, w_scales, gate, offs, pos1, pos2, out):
    nc = tc.nc
    with ExitStack() as ctx:
        lists = ctx.enter_context(tc.tile_pool(name="lists", bufs=1))
        keep = ctx.enter_context(tc.tile_pool(name="keep", bufs=1))
        psum = ctx.enter_context(tc.psum_pool(name="psum", bufs=1))

        offs_t = lists.tile([P, SLOTS // 16], U16, name="offs_t")
        pos_t = [lists.tile([P, T // 16], U16, name="pos%d_t" % r) for r in range(2)]

        tok_bytes = keep.tile([P, T], U8, name="tok_bytes", align_bytes=64)
        nc.gpsimd.memset(tok_bytes[:], 0)
        ws = keep.tile([P, E * PASSES // W_PLANES, N], U8, name="ws", align_bytes=64)
        nc.vector.memset(ws[:].rearrange("p g n -> p (g n)").bitcast(I32), 0)
        ident = keep.tile([P, P], F32, name="ident")
        make_identity(nc, ident[:])
        gate_rows = keep.tile([P, P], F32, name="gate_rows")
        nc.gpsimd.memset(gate_rows[:], 0.0)

        x_view = xT.rearrange("(a p j) t -> a p j t", p=P, j=PACK)
        raw = {}
        for a in range(PASSES):
            t0 = 0
            for n in X_LOADS[a]:
                chunk = keep.tile([P, PACK, n], F32, name="raw%d_%d" % (a, t0))
                nc.sync.dma_start(chunk[:], x_view[a][:, :, t0:t0 + n])
                raw[a, t0] = chunk
                t0 += n
            if a == 0:
                nc.sync.dma_start(offs_t[:], offs)

        for r in range(2):
            nc.sync.dma_start(gate_rows[GATE_ROWS * r:GATE_ROWS * (r + 1), :], gate[r, 0, :].rearrange("(h c) -> h c", c=P))

        s_view = w_scales.rearrange("(g f) a (q r) n -> (f a) r q g n", f=2, r=4)
        for r in (0, 2, 1, 3):
            for f in range(W_PLANES):
                nc.sync.dma_start(ws[4 * f + r:P:32, :, :].bitcast(I32), s_view[f, r].bitcast(I32))

        codes = {}

        def load_codes(e0, e1, n0, n1):
            tile_ = keep.tile([P, (e1 - e0) * PASSES, n1 - n0], I32, name="w%d_%d" % (e0, n0), align_bytes=64)
            nc.sync.dma_start(
                tile_[:],
                w_words[e0:e1, :, :, n0:n1, :].rearrange("e a p n r -> p (e a) (n r)").bitcast(I32),
            )
            for e in range(e0, e1):
                for b in range(n0 // P, n1 // P):
                    for a in range(PASSES):
                        codes[b, e, a] = tile_[:, (e - e0) * PASSES + a, b * P - n0:(b + 1) * P - n0]

        for e0, e1 in W_BOTH:
            load_codes(e0, e1, 0, N)
        for e0, e1 in W_BLOCK0:
            load_codes(e0, e1, 0, P)
        nc.sync.dma_start(pos_t[0][:], pos1)
        nc.sync.dma_start(pos_t[1][:], pos2)
        for e0, e1 in W_BLOCK1:
            load_codes(e0, e1, P, N)

        tok_words = [keep.tile([P, T], U32, name="tok_words%d" % a, align_bytes=64) for a in range(PASSES)]

        def raw_tokens(a, t0, n):
            first = max(t for b, t in raw if b == a and t <= t0)
            return raw[a, first][:, :, t0 - first:t0 - first + n]

        def quantise_pass(a):
            t0 = 0
            for copies in QUANT[a]:
                wide = sum(n for n, by_vector in copies)
                grouped = keep.tile([P, wide, PACK], BF16, name="grouped%d_%d" % (a, t0), align_bytes=64)
                done = 0
                for n, by_vector in copies:
                    src = raw_tokens(a, t0 + done, n).rearrange("p j (c i) -> p c j i", i=4)
                    dst = grouped[:, done:done + n, :].rearrange("p (c i) j -> p c j i", i=4)
                    cut = by_vector // 4
                    if by_vector > 0:
                        nc.vector.tensor_copy(out=dst[:, :cut], in_=src[:, :cut])
                    if by_vector < n:
                        nc.scalar.copy(out=dst[:, cut:], in_=src[:, cut:])
                    done += n
                cols = slice(t0, t0 + wide)
                nc.vector.quantize_mx(
                    out=tok_words[a][:, cols].bitcast(FP8X4),
                    scales=tok_bytes[PLANE[a]:P, cols],
                    in_=grouped[:].rearrange("p t j -> p (t j)"),
                )
                t0 += wide

        starts = [sum(SLICES[:s]) for s in range(len(SLICES))]
        slice_of = [max(s for s in range(len(SLICES)) if starts[s] <= e * C) for e in range(E)]
        gw = {}
        gb = {}

        def gather_words(a, s, cuts):
            for i, cut in enumerate(cuts):
                lo = starts[s] + sum(cuts[:i])
                piece = keep.tile([P, cut], U32, name="gw%d_%d" % (a, lo), align_bytes=64)
                nc.vector.tensor_copy(piece[:], tok_words[a][:].indirect(offs_t[:, lo // 16:(lo + cut) // 16]))
                for e in range(lo // C, (lo + cut) // C):
                    gw[a, e] = piece[:, e * C - lo:(e + 1) * C - lo]

        def gather_bytes(s):
            gb[s] = keep.tile([P, SLICES[s]], U8, name="gb%d" % s, align_bytes=64)
            lcols = slice(starts[s] // 16, (starts[s] + SLICES[s]) // 16)
            nc.vector.tensor_copy(gb[s][:], tok_bytes[:].indirect(offs_t[:, lcols]))

        def multiply(b, e, a, dst):
            s = slice_of[e]
            o = e * C - starts[s]
            nc.tensor.matmul_mx(
                out=dst,
                lhsT=codes[b, e, a].bitcast(FP8X4),
                lhsT_scale=ws[4 * (PASSES * (e % 2) + a):P, e // 2, b * P:(b + 1) * P],
                rhs=gw[a, e].bitcast(FP8X4),
                rhs_scale=gb[s][PLANE[a]:P, o:o + C],
                start=(a == 0),
                stop=(a == PASSES - 1),
            )

        quantise_pass(0)
        for s in range(len(SLICES)):
            gather_words(0, s, (SLICES[s],))
        quantise_pass(1)

        gate_cols = keep.tile([P, 2 * GATE_ROWS], F32, name="gate_cols")
        turned = psum.tile([P, P], F32, name="spare0")
        nc.tensor.transpose(turned[:], gate_rows[:], ident[:])
        nc.scalar.copy(out=gate_cols[:], in_=turned[:, 0:2 * GATE_ROWS])
        gt = [keep.tile([P, T], F32, name="gate%d" % r) for r in range(2)]
        for q in range(2 * T // BANK):
            spread = psum.tile([P, BANK], F32, name="spare%d" % ((q + 1) % 2))
            for i in range(BANK // P):
                m = q * (BANK // P) + i
                nc.tensor.transpose(spread[:, i * P:(i + 1) * P], gate_cols[:, m:m + 1].to_broadcast([P, P]), ident[:])
            nc.scalar.copy(out=gt[q * BANK // T][:, q * BANK % T:q * BANK % T + BANK], in_=spread[:])

        y_sb = [keep.tile([P, SLOTS], F32, name="y_sb%d" % b) for b in range(2)]

        acc = [psum.tile([P, PER_BANK, C], F32, name="acc%d" % i) for i in range(NBANK)]
        y0_view = y_sb[0][:].rearrange("p (g i c) -> p i g c", i=NBANK, c=C)
        last = len(SLICES) - 1
        early = [psum.tile([P, PER_BANK, C], F32, name="early%d" % i) for i in range(EARLY // PER_BANK)]
        for s in range(len(SLICES)):
            experts = [e for e in range(E) if slice_of[e] == s]
            gather_bytes(s)
            if s == last:
                for e in experts:
                    multiply(0, e, 0, acc[e % NBANK][:, e // NBANK, :])
            gather_words(1, s, LAST_CUTS if s == last else (SLICES[s],))
            for e in experts:
                for a in range(PASSES):
                    if s != last or a > 0:
                        multiply(0, e, a, acc[e % NBANK][:, e // NBANK, :])
            order = sorted(range(NBANK), key=lambda i: max(e for e in experts if e % NBANK == i))
            for n, i in enumerate(order):
                groups = [e // NBANK for e in experts if e % NBANK == i]
                g0, g1 = min(groups), max(groups) + 1
                if s == last and n == NBANK - 1:
                    nc.vector.tensor_copy(out=y0_view[:, i, g0:g1, :], in_=acc[i][:, g0:g1, :])
                else:
                    nc.scalar.copy(out=y0_view[:, i, g0:g1, :], in_=acc[i][:, g0:g1, :])
            soon = [e for e in experts if e < EARLY]
            for e in soon:
                for a in range(PASSES):
                    multiply(1, e, a, early[e // PER_BANK][:, e % PER_BANK, :])
            for i in range(len(early)):
                mine = [e for e in soon if e // PER_BANK == i]
                if mine:
                    nc.scalar.copy(
                        out=y_sb[1][:, mine[0] * C:(mine[-1] + 1) * C],
                        in_=early[i][:, mine[0] % PER_BANK:mine[-1] % PER_BANK + 1, :].rearrange("p g c -> p (g c)"),
                    )

        acc1 = [None, None] + [psum.tile([P, PER_BANK, C], F32, name="acc%d" % i) for i in (2, 3)]
        for e0, e1, i, g in RUNS1:
            for e in range(e0, e1):
                for a in range(PASSES):
                    multiply(1, e, a, acc1[i][:, g + e - e0, :])
            nc.scalar.copy(
                out=y_sb[1][:, e0 * C:e1 * C],
                in_=acc1[i][:, g:g + e1 - e0, :].rearrange("p g c -> p (g c)"),
            )

        def fetch(b, r, t0, n):
            part = keep.tile([P, n], F32, name="part%d_%d_%d" % (b, r, t0))
            nc.vector.tensor_tensor(
                out=part[:],
                in0=y_sb[b][:].indirect(pos_t[r][:, t0 // 16:(t0 + n) // 16]),
                in1=gt[r][:, t0:t0 + n],
                op=MULT,
            )
            return part

        def add_product(total, part, r):
            nc.tensor.matmul(out=total[:], lhsT=ident[:], rhs=part, start=(r == 0), stop=(r == 1))

        def store_total(total, b, t0, n):
            res = keep.tile([P, n], F32, name="res%d_%d" % (b, t0))
            nc.scalar.copy(out=res[:], in_=total[:])
            nc.scalar.dma_start(out[b * P:(b + 1) * P, t0:t0 + n], res[:])

        halves = range(0, T, BANK)
        total0 = {t0: psum.tile([P, BANK], F32, name="acc%d" % (NBANK - 2 + t0 // BANK)) for t0 in halves}
        for r in range(2):
            for t0 in halves:
                add_product(total0[t0], fetch(0, r, t0, BANK)[:], r)
        for t0 in halves:
            store_total(total0[t0], 0, t0, BANK)

        total1 = psum.tile([P, SUM1], F32, name="spare0")
        for r in range(2):
            add_product(total1, fetch(1, r, 0, SUM1)[:], r)
        store_total(total1, 1, 0, SUM1)
        first = fetch(1, 0, SUM1, T - SUM1)
        cuts = [(SUM1 + sum(CHUNKS1[:i]), n) for i, n in enumerate(CHUNKS1)]
        second = [fetch(1, 1, t0, n) for t0, n in cuts]
        for (t0, n), part in zip(cuts, second):
            res = keep.tile([P, n], F32, name="res1_%d" % t0)
            nc.vector.tensor_tensor(out=res[:], in0=first[:, t0 - SUM1:t0 - SUM1 + n], in1=part[:], op=ADD)
            nc.sync.dma_start(out[P:2 * P, t0:t0 + n], res[:])
